import numpy as np
import ml_dtypes


def mxq(x, axis, fmt="e4m3"):
    dtype, down = {"e4m3": (ml_dtypes.float8_e4m3fn, 7), "e5m2": (ml_dtypes.float8_e5m2, 14)}[fmt]
    v = np.moveaxis(np.asarray(x, np.float32).astype(ml_dtypes.bfloat16).astype(np.float64), axis, -1)
    blocks = v.reshape(v.shape[:-1] + (-1, 32))
    amax = np.abs(blocks).max(-1, keepdims=True)
    byte = np.maximum(np.where(amax > 0, np.frexp(amax)[1] - 1 + 127, 0) - down, 1)
    scale = np.exp2(byte - 127.0)
    codes = (blocks / scale).astype(np.float32).astype(dtype).astype(np.float64)
    return np.moveaxis((codes * scale).reshape(v.shape), -1, axis)


WIDE = False


def mx_kscale(k, group=512):
    if not WIDE:
        return np.ones(k)
    levels = np.array([18, -18])
    if group != 512:
        return np.exp2(np.random.permutation(np.resize(levels, k // group))).repeat(group)
    if k % 512:
        return np.exp2(np.random.permutation(np.resize(levels, k // 32))).repeat(32)
    a = np.empty((k // 512, 16))
    for p in range(k // 512):
        a[p, :8] = np.random.permutation(np.resize(levels, 8))
        for g in range(8):
            far = levels[np.abs(levels - a[p, g]) >= 10]
            a[p, g + 8] = far[np.random.randint(len(far))]
    return np.exp2(a.ravel()).repeat(32)


def f64(x):
    return np.asarray(x).astype(np.float64)


def softplus(v):
    return np.log(1.0 + np.exp(v))


def sigmoid(v):
    return 1.0 / (1.0 + np.exp(-v))


G, D, M, O, N = 4, 128, 128, 128, 512


def setup_inputs():
    n = np.random.standard_normal
    s_d = mx_kscale(D, 0)
    s_o = mx_kscale(O, 0)
    return {
        "x": (n((G, D, N)) * s_d[:, None]).astype(np.float32),
        "w1": (n((G, D, M)) / np.sqrt(D) / s_d[:, None]).astype(np.float32),
        "w2": (n((G, D, M)) / np.sqrt(D) / s_d[:, None]).astype(np.float32),
        "hp1": (np.random.uniform(0.3, 1.0, (G, M, 1))).astype(np.float32),
        "wo": (n((G, O, M)) / np.sqrt(O) / s_o[:, None]).astype(np.float32),
        "dy": (n((G, O, N)) * s_o[:, None]).astype(np.float32),
        "old": (0.3 * n((G, M, N))).astype(np.float32),
    }


def reference(x, w1, w2, hp1, wo, dy, old):
    w1q = mxq(f64(w1), 1, "e4m3")
    xq = mxq(f64(x), 1, "e4m3")
    z1 = w1q.transpose(0, 2, 1) @ xq
    w2q = mxq(f64(w2), 1, "e4m3")
    z2 = w2q.transpose(0, 2, 1) @ xq
    q1 = np.square(softplus(z1))
    woq = mxq(f64(wo), 1, "e4m3")
    dyq = mxq(f64(dy), 1, "e4m3")
    c0 = woq.transpose(0, 2, 1) @ dyq
    dq1 = c0 * 2.0 / (q1 + softplus(z2) + f64(hp1)) - c0 * 2.0 * q1 / np.square(q1 + softplus(z2) + f64(hp1))
    dz1 = dq1 * softplus(z1) * 2.0 * sigmoid(z1)
    y = dz1 + f64(old)
    return y

@@ -1,0 +1,235 @@
+from contextlib import ExitStack
+import math
+
+import concourse.mybir as mybir
+
+G, D, M, N = 4, 128, 128, 512
+FLOPS = 3 * 2 * G * D * M * N
+
+F32 = mybir.dt.float32
+BF16 = mybir.dt.bfloat16
+U32 = mybir.dt.uint32
+U8 = mybir.dt.uint8
+FP8X4 = mybir.dt.float8_e4m3fn_x4
+ACT = mybir.ActivationFunctionType
+ALU = mybir.AluOpType
+
+P = 128
+PACK = 4
+ROWS = D // PACK
+HALF = N // 2
+NT = 128
+RUN = 4
+TINY = 2.0 ** -44
+SCALAR_EVAC = (3,)
+
+
+def tile_rows_bhill_kernel(tc, x, w1, w2, hp1, wo, dy, old, out):
+    nc = tc.nc
+
+    with ExitStack() as ctx:
+        sb = ctx.enter_context(tc.tile_pool(name="sb", bufs=1))
+        ps = ctx.enter_context(tc.psum_pool(name="ps", bufs=1))
+        ctx.enter_context(tc.manual_schedule())
+
+        def load(name, src):
+            width = src.shape[2]
+            raw = sb.tile([P, PACK, width], F32, name=name)
+            nc.sync.dma_start(out=raw[:], in_=src.rearrange("g (p j) c -> (g p) j c", j=PACK))
+            return raw
+
+        def interleave(dst, raw):
+            nc.vector.tensor_copy(
+                out=dst.rearrange("p (c i) j -> p c j i", i=RUN),
+                in_=raw.rearrange("p j (c i) -> p c j i", i=RUN),
+            )
+
+        def quantize(codes, scales, packed):
+            nc.vector.quantize_mx(
+                out=codes.bitcast(FP8X4), scales=scales, in_=packed.rearrange("p c j -> p (c j)")
+            )
+
+        def operand(name, width):
+            packed = sb.tile([P, width, PACK], BF16, name=name + "_bf", align_bytes=64)
+            codes = sb.tile([P, width], U32, name=name + "_codes", align_bytes=64)
+            scales = sb.tile([P, width], U8, name=name + "_scales", align_bytes=64)
+            return packed, codes, scales
+
+        def product(dst, g, w_codes, w_scales, w_cols, a_codes, a_scales, a_cols):
+            rows = slice(ROWS * g, ROWS * (g + 1))
+            nc.tensor.matmul_mx(
+                out=dst,
+                lhsT=w_codes[rows, w_cols].bitcast(FP8X4),
+                lhsT_scale=w_scales[rows, w_cols],
+                rhs=a_codes[rows, a_cols].bitcast(FP8X4),
+                rhs_scale=a_scales[rows, a_cols],
+                start=True,
+                stop=True,
+            )
+
+        def per_group(name, shape):
+            return [sb.tile(shape, F32, name="%s%d" % (name, g)) for g in range(G)]
+
+        w1_raw = load("w1_raw", w1)
+        w2_raw = load("w2_raw", w2)
+        x_raw = [load("x_raw%d" % h, x[:, :, h * HALF : (h + 1) * HALF]) for h in range(2)]
+        wo_raw = load("wo_raw", wo)
+        dy_raw = load("dy_raw", dy)
+        hp = sb.tile([P, G], F32, name="hp")
+        with nc.allow_non_contiguous_dma(reason="one half point to a partition"):
+            nc.sync.dma_start(out=hp[:], in_=hp1.rearrange("g m one -> m (g one)"))
+        old_sb = sb.tile([P, G, N], F32, name="old_sb")
+        nc.sync.dma_start(out=old_sb[:], in_=old.rearrange("g m n -> m g n"))
+
+        w12_bf, w12_codes, w12_scales = operand("w12", 2 * M)
+        x_ops = [operand("x%d" % h, HALF) for h in range(2)]
+        wo_bf, wo_codes, wo_scales = operand("wo", M)
+        dy_bf, dy_codes, dy_scales = operand("dy", N)
+
+        banks = [[ps.tile([P, N], F32, name="bank%d_%d" % (h, g)) for g in range(G)] for h in range(2)]
+        wide = [P, 2, 2, HALF]
+        flat = [P, 2, HALF]
+        sn = per_group("sn", wide)
+        z_kept = per_group("z_kept", [P, N])
+        logs = per_group("logs", wide)
+        soft = per_group("soft", wide)
+        sq = per_group("sq", flat)
+        den = per_group("den", flat)
+        log_den = per_group("log_den", flat)
+        inv2 = per_group("inv2", flat)
+        gate = per_group("gate", flat)
+        num = per_group("num", flat)
+        num2 = per_group("num2", flat)
+        grad = per_group("grad", flat)
+        res = per_group("res", flat)
+
+        def row(t):
+            return t.rearrange("p k c -> p (k c)")
+
+        interleave(w12_bf[:, 0:M, :], w1_raw[:])
+        interleave(w12_bf[:, M : 2 * M, :], w2_raw[:])
+        quantize(w12_codes[:], w12_scales[:], w12_bf[:])
+
+        def forward(h):
+            x_bf, x_codes, x_scales = x_ops[h]
+            parts = [slice(i * NT, (i + 1) * NT) for i in range(HALF // NT)]
+            for cols in parts:
+                interleave(x_bf[:, cols, :], x_raw[h][:, :, cols])
+            for cols in parts:
+                quantize(x_codes[:, cols], x_scales[:, cols], x_bf[:, cols, :])
+            for g in range(G):
+                for cols in parts:
+                    for k in range(2):
+                        dst = banks[h][g][:, k * HALF + cols.start : k * HALF + cols.stop]
+                        product(dst, g, w12_codes, w12_scales, slice(k * M, (k + 1) * M), x_codes, x_scales, cols)
+
+        def sigmoid(h, g):
+            nc.scalar.activation(out=row(sn[g][:, h]), in_=banks[h][g][:], func=ACT.Sigmoid, scale=-1.0)
+
+        def keep_z(g):
+            if g in SCALAR_EVAC:
+                nc.scalar.copy(out=z_kept[g][:], in_=banks[0][g][:])
+            else:
+                nc.vector.tensor_copy(out=z_kept[g][:], in_=banks[0][g][:])
+
+        def backward(g):
+            for i in range(N // NT):
+                cols = slice(i * NT, (i + 1) * NT)
+                product(banks[0][g][:, cols], g, wo_codes, wo_scales, slice(0, M), dy_codes, dy_scales, cols)
+
+        forward(0)
+        for g in range(G):
+            sigmoid(0, g)
+        keep_z(3)
+        forward(1)
+        for g in range(G):
+            sigmoid(1, g)
+        keep_z(0)
+        interleave(wo_bf[:], wo_raw[:])
+        keep_z(1)
+        quantize(wo_codes[:], wo_scales[:], wo_bf[:])
+        halves = [slice(h * HALF, (h + 1) * HALF) for h in range(2)]
+        for cols in halves:
+            interleave(dy_bf[:, cols, :], dy_raw[:, :, cols])
+        for cols in halves:
+            quantize(dy_codes[:, cols], dy_scales[:, cols], dy_bf[:, cols, :])
+        keep_z(2)
+        for g in range(G):
+            backward(g)
+
+        def take_log(g, h):
+            nc.scalar.activation(out=row(logs[g][:, h]), in_=row(sn[g][:, h]), func=ACT.Ln, bias=TINY)
+
+        def softplus(g, h):
+            z = z_kept[g][:] if h == 0 else banks[1][g][:]
+            nc.vector.scalar_tensor_tensor(
+                out=row(soft[g][:, h]), in0=row(logs[g][:, h]), scalar=-1.0, in1=z, op0=ALU.mult, op1=ALU.max
+            )
+
+        def make_gate(g):
+            nc.vector.scalar_tensor_tensor(
+                out=gate[g][:], in0=sn[g][:, :, 0, :], scalar=1.0,
+                in1=banks[0][g][:].rearrange("p (h c) -> p h c", h=2), op0=ALU.subtract, op1=ALU.mult,
+            )
+
+        def square(g):
+            nc.scalar.activation(out=sq[g][:], in_=soft[g][:, :, 0, :], func=ACT.Square)
+
+        def make_den(g):
+            nc.vector.scalar_tensor_tensor(
+                out=den[g][:], in0=soft[g][:, :, 1, :], scalar=hp[:, g : g + 1], in1=sq[g][:],
+                op0=ALU.add, op1=ALU.add,
+            )
+
+        def take_log_den(g):
+            nc.scalar.activation(out=row(log_den[g][:]), in_=row(den[g][:]), func=ACT.Ln)
+
+        def make_num(g):
+            nc.vector.scalar_tensor_tensor(
+                out=num[g][:], in0=soft[g][:, :, 1, :], scalar=hp[:, g : g + 1], in1=soft[g][:, :, 0, :],
+                op0=ALU.add, op1=ALU.mult,
+            )
+
+        def make_num2(g):
+            nc.vector.tensor_tensor(out=row(num2[g][:]), in0=row(num[g][:]), in1=row(gate[g][:]), op=ALU.mult)
+
+        def inverse_square(g):
+            nc.scalar.activation(
+                out=row(inv2[g][:]), in_=row(log_den[g][:]), func=ACT.Exp, scale=-2.0, bias=math.log(4.0)
+            )
+
+        def make_grad(g):
+            nc.vector.tensor_tensor(out=row(grad[g][:]), in0=row(num2[g][:]), in1=row(inv2[g][:]), op=ALU.mult)
+
+        def finish(g, cols):
+            nc.vector.tensor_tensor(
+                out=row(res[g][:])[:, cols], in0=old_sb[:, g, cols], in1=row(grad[g][:])[:, cols], op=ALU.subtract
+            )
+            nc.sync.dma_start(out=out[g, :, cols], in_=row(res[g][:])[:, cols])
+
+        for g in range(G):
+            make_gate(g)
+        for g in range(G):
+            for h in range(2):
+                take_log(g, h)
+                softplus(g, h)
+            if g >= 1:
+                square(g - 1)
+                make_den(g - 1)
+            if g >= 2:
+                take_log_den(g - 2)
+                make_num(g - 2)
+        square(G - 1)
+        make_den(G - 1)
+        for g in range(G - 2, G):
+            take_log_den(g)
+            make_num(g)
+        for g in range(G):
+            make_num2(g)
+            inverse_square(g)
+        make_grad(0)
+        for g in range(G - 1):
+            make_grad(g + 1)
+            finish(g, slice(0, N))
+        for cols in halves:
+            finish(G - 1, cols)

@@ -21,7 +21,6 @@ HALF = N // 2
 NT = 128
 RUN = 4
 TINY = 2.0 ** -44
-SCALAR_EVAC = (3,)
 
 
 def tile_rows_bhill_kernel(tc, x, w1, w2, hp1, wo, dy, old, out):
@@ -70,9 +69,12 @@ def tile_rows_bhill_kernel(tc, x, w1, w2, hp1, wo, dy, old, out):
         def per_group(name, shape):
             return [sb.tile(shape, F32, name="%s%d" % (name, g)) for g in range(G)]
 
-        w1_raw = load("w1_raw", w1)
-        w2_raw = load("w2_raw", w2)
-        x_raw = [load("x_raw%d" % h, x[:, :, h * HALF : (h + 1) * HALF]) for h in range(2)]
+        halves = [slice(h * HALF, (h + 1) * HALF) for h in range(2)]
+        w_raw = [None, None]
+        x_raw = [None, None]
+        for i, w in enumerate((w1, w2)):
+            w_raw[i] = load("w_raw%d" % i, w)
+            x_raw[i] = load("x_raw%d" % i, x[:, :, halves[i]])
         wo_raw = load("wo_raw", wo)
         dy_raw = load("dy_raw", dy)
         hp = sb.tile([P, G], F32, name="hp")
@@ -81,7 +83,7 @@ def tile_rows_bhill_kernel(tc, x, w1, w2, hp1, wo, dy, old, out):
         old_sb = sb.tile([P, G, N], F32, name="old_sb")
         nc.sync.dma_start(out=old_sb[:], in_=old.rearrange("g m n -> m g n"))
 
-        w12_bf, w12_codes, w12_scales = operand("w12", 2 * M)
+        w_ops = [operand("w%d" % i, M) for i in range(2)]
         x_ops = [operand("x%d" % h, HALF) for h in range(2)]
         wo_bf, wo_codes, wo_scales = operand("wo", M)
         dy_bf, dy_codes, dy_scales = operand("dy", N)
@@ -90,7 +92,6 @@ def tile_rows_bhill_kernel(tc, x, w1, w2, hp1, wo, dy, old, out):
         wide = [P, 2, 2, HALF]
         flat = [P, 2, HALF]
         sn = per_group("sn", wide)
-        z_kept = per_group("z_kept", [P, N])
         logs = per_group("logs", wide)
         soft = per_group("soft", wide)
         sq = per_group("sq", flat)
@@ -106,54 +107,47 @@ def tile_rows_bhill_kernel(tc, x, w1, w2, hp1, wo, dy, old, out):
         def row(t):
             return t.rearrange("p k c -> p (k c)")
 
-        interleave(w12_bf[:, 0:M, :], w1_raw[:])
-        interleave(w12_bf[:, M : 2 * M, :], w2_raw[:])
-        quantize(w12_codes[:], w12_scales[:], w12_bf[:])
+        parts = [slice(i * NT, (i + 1) * NT) for i in range(HALF // NT)]
 
-        def forward(h):
+        def prepare_x(h):
             x_bf, x_codes, x_scales = x_ops[h]
-            parts = [slice(i * NT, (i + 1) * NT) for i in range(HALF // NT)]
             for cols in parts:
                 interleave(x_bf[:, cols, :], x_raw[h][:, :, cols])
             for cols in parts:
                 quantize(x_codes[:, cols], x_scales[:, cols], x_bf[:, cols, :])
-            for g in range(G):
-                for cols in parts:
-                    for k in range(2):
-                        dst = banks[h][g][:, k * HALF + cols.start : k * HALF + cols.stop]
-                        product(dst, g, w12_codes, w12_scales, slice(k * M, (k + 1) * M), x_codes, x_scales, cols)
 
-        def sigmoid(h, g):
-            nc.scalar.activation(out=row(sn[g][:, h]), in_=banks[h][g][:], func=ACT.Sigmoid, scale=-1.0)
-
-        def keep_z(g):
-            if g in SCALAR_EVAC:
-                nc.scalar.copy(out=z_kept[g][:], in_=banks[0][g][:])
-            else:
-                nc.vector.tensor_copy(out=z_kept[g][:], in_=banks[0][g][:])
+        def forward(h, g, k):
+            for cols in parts:
+                dst = banks[h][g][:, k * HALF + cols.start : k * HALF + cols.stop]
+                product(dst, g, w_ops[k][1], w_ops[k][2], slice(0, M), x_ops[h][1], x_ops[h][2], cols)
 
         def backward(g):
             for i in range(N // NT):
                 cols = slice(i * NT, (i + 1) * NT)
                 product(banks[0][g][:, cols], g, wo_codes, wo_scales, slice(0, M), dy_codes, dy_scales, cols)
 
-        forward(0)
+        interleave(w_ops[0][0][:], w_raw[0][:])
+        quantize(w_ops[0][1][:], w_ops[0][2][:], w_ops[0][0][:])
+        prepare_x(0)
+        interleave(w_ops[1][0][:], w_raw[1][:])
+        quantize(w_ops[1][1][:], w_ops[1][2][:], w_ops[1][0][:])
+        for k in range(2):
+            for g in range(G):
+                forward(0, g, k)
+                nc.scalar.activation(
+                    out=sn[g][:, 0, k, :], in_=banks[0][g][:, halves[k]], func=ACT.Sigmoid, scale=-1.0
+                )
+        prepare_x(1)
         for g in range(G):
-            sigmoid(0, g)
-        keep_z(3)
-        forward(1)
-        for g in range(G):
-            sigmoid(1, g)
-        keep_z(0)
+            for k in range(2):
+                forward(1, g, k)
+            nc.scalar.activation(out=row(sn[g][:, 1]), in_=banks[1][g][:], func=ACT.Sigmoid, scale=-1.0)
         interleave(wo_bf[:], wo_raw[:])
-        keep_z(1)
         quantize(wo_codes[:], wo_scales[:], wo_bf[:])
-        halves = [slice(h * HALF, (h + 1) * HALF) for h in range(2)]
         for cols in halves:
             interleave(dy_bf[:, cols, :], dy_raw[:, :, cols])
         for cols in halves:
             quantize(dy_codes[:, cols], dy_scales[:, cols], dy_bf[:, cols, :])
-        keep_z(2)
         for g in range(G):
             backward(g)
 
@@ -161,7 +155,7 @@ def tile_rows_bhill_kernel(tc, x, w1, w2, hp1, wo, dy, old, out):
             nc.scalar.activation(out=row(logs[g][:, h]), in_=row(sn[g][:, h]), func=ACT.Ln, bias=TINY)
 
         def softplus(g, h):
-            z = z_kept[g][:] if h == 0 else banks[1][g][:]
+            z = banks[h][g][:]
             nc.vector.scalar_tensor_tensor(
                 out=row(soft[g][:, h]), in0=row(logs[g][:, h]), scalar=-1.0, in1=z, op0=ALU.mult, op1=ALU.max
             )
@@ -184,14 +178,14 @@ def tile_rows_bhill_kernel(tc, x, w1, w2, hp1, wo, dy, old, out):
         def take_log_den(g):
             nc.scalar.activation(out=row(log_den[g][:]), in_=row(den[g][:]), func=ACT.Ln)
 
-        def make_num(g):
-            nc.vector.scalar_tensor_tensor(
-                out=num[g][:], in0=soft[g][:, :, 1, :], scalar=hp[:, g : g + 1], in1=soft[g][:, :, 0, :],
-                op0=ALU.add, op1=ALU.mult,
-            )
+        def make_num(g, engine):
+            engine.tensor_tensor(out=num[g][:], in0=soft[g][:, :, 0, :], in1=gate[g][:], op=ALU.mult)
 
         def make_num2(g):
-            nc.vector.tensor_tensor(out=row(num2[g][:]), in0=row(num[g][:]), in1=row(gate[g][:]), op=ALU.mult)
+            nc.vector.scalar_tensor_tensor(
+                out=num2[g][:], in0=soft[g][:, :, 1, :], scalar=hp[:, g : g + 1], in1=num[g][:],
+                op0=ALU.add, op1=ALU.mult,
+            )
 
         def inverse_square(g):
             nc.scalar.activation(
@@ -209,21 +203,24 @@ def tile_rows_bhill_kernel(tc, x, w1, w2, hp1, wo, dy, old, out):
 
         for g in range(G):
             make_gate(g)
+            for k in range(2):
+                forward(0, g, k)
+        last = G - 1
         for g in range(G):
-            for h in range(2):
+            for h in (1, 0):
                 take_log(g, h)
                 softplus(g, h)
-            if g >= 1:
-                square(g - 1)
-                make_den(g - 1)
-            if g >= 2:
-                take_log_den(g - 2)
-                make_num(g - 2)
-        square(G - 1)
-        make_den(G - 1)
-        for g in range(G - 2, G):
+            if g < last:
+                make_num(g, nc.gpsimd)
+        for g in range(last):
+            square(g)
+        nc.vector.tensor_tensor(
+            out=sq[last][:], in0=soft[last][:, :, 0, :], in1=soft[last][:, :, 0, :], op=ALU.mult
+        )
+        for g in range(G):
+            make_den(g)
             take_log_den(g)
-            make_num(g)
+        make_num(last, nc.vector)
         for g in range(G):
             make_num2(g)
             inverse_square(g)

@@ -18,7 +18,6 @@ P = 128
 PACK = 4
 ROWS = D // PACK
 HALF = N // 2
-NT = 128
 RUN = 4
 TINY = 2.0 ** -44
 
@@ -33,190 +32,136 @@ def tile_rows_bhill_kernel(tc, x, w1, w2, hp1, wo, dy, old, out):
 
         def load(name, src):
             width = src.shape[2]
-            raw = sb.tile([P, PACK, width], F32, name=name)
+            raw = sb.tile([P, PACK, width], F32, name=name + "_raw")
             nc.sync.dma_start(out=raw[:], in_=src.rearrange("g (p j) c -> (g p) j c", j=PACK))
-            return raw
-
-        def interleave(dst, raw):
-            nc.vector.tensor_copy(
-                out=dst.rearrange("p (c i) j -> p c j i", i=RUN),
-                in_=raw.rearrange("p j (c i) -> p c j i", i=RUN),
-            )
-
-        def quantize(codes, scales, packed):
-            nc.vector.quantize_mx(
-                out=codes.bitcast(FP8X4), scales=scales, in_=packed.rearrange("p c j -> p (c j)")
-            )
-
-        def operand(name, width):
             packed = sb.tile([P, width, PACK], BF16, name=name + "_bf", align_bytes=64)
             codes = sb.tile([P, width], U32, name=name + "_codes", align_bytes=64)
             scales = sb.tile([P, width], U8, name=name + "_scales", align_bytes=64)
-            return packed, codes, scales
+            return {"raw": raw, "packed": packed, "codes": codes, "scales": scales, "all": slice(0, width)}
 
-        def product(dst, g, w_codes, w_scales, w_cols, a_codes, a_scales, a_cols):
+        def interleave(copy, op, cols):
+            copy(
+                out=op["packed"][:, cols, :].rearrange("p (c i) j -> p c j i", i=RUN),
+                in_=op["raw"][:, :, cols].rearrange("p j (c i) -> p c j i", i=RUN),
+            )
+
+        def quantize(op, cols):
+            nc.vector.quantize_mx(
+                out=op["codes"][:, cols].bitcast(FP8X4),
+                scales=op["scales"][:, cols],
+                in_=op["packed"][:, cols, :].rearrange("p c j -> p (c j)"),
+            )
+
+        def product(bank, g, weights, moving):
             rows = slice(ROWS * g, ROWS * (g + 1))
             nc.tensor.matmul_mx(
-                out=dst,
-                lhsT=w_codes[rows, w_cols].bitcast(FP8X4),
-                lhsT_scale=w_scales[rows, w_cols],
-                rhs=a_codes[rows, a_cols].bitcast(FP8X4),
-                rhs_scale=a_scales[rows, a_cols],
+                out=bank[:],
+                lhsT=weights["codes"][rows, :].bitcast(FP8X4),
+                lhsT_scale=weights["scales"][rows, :],
+                rhs=moving["codes"][rows, :].bitcast(FP8X4),
+                rhs_scale=moving["scales"][rows, :],
                 start=True,
                 stop=True,
             )
 
-        def per_group(name, shape):
-            return [sb.tile(shape, F32, name="%s%d" % (name, g)) for g in range(G)]
+        def per_group(name):
+            return [sb.tile([P, N], F32, name="%s%d" % (name, g)) for g in range(G)]
 
-        halves = [slice(h * HALF, (h + 1) * HALF) for h in range(2)]
-        w_raw = [None, None]
-        x_raw = [None, None]
-        for i, w in enumerate((w1, w2)):
-            w_raw[i] = load("w_raw%d" % i, w)
-            x_raw[i] = load("x_raw%d" % i, x[:, :, halves[i]])
-        wo_raw = load("wo_raw", wo)
-        dy_raw = load("dy_raw", dy)
+        x_op = load("x", x)
+        w1_op = load("w1", w1)
+        w2_op = load("w2", w2)
+        wo_op = load("wo", wo)
+        dy_op = load("dy", dy)
         hp = sb.tile([P, G], F32, name="hp")
         with nc.allow_non_contiguous_dma(reason="one half point to a partition"):
             nc.sync.dma_start(out=hp[:], in_=hp1.rearrange("g m one -> m (g one)"))
         old_sb = sb.tile([P, G, N], F32, name="old_sb")
         nc.sync.dma_start(out=old_sb[:], in_=old.rearrange("g m n -> m g n"))
 
-        w_ops = [operand("w%d" % i, M) for i in range(2)]
-        x_ops = [operand("x%d" % h, HALF) for h in range(2)]
-        wo_bf, wo_codes, wo_scales = operand("wo", M)
-        dy_bf, dy_codes, dy_scales = operand("dy", N)
+        banks = [[ps.tile([P, N], F32, name="bank%d_%d" % (k, g)) for g in range(G)] for k in range(2)]
+        sn = [per_group("sn1_"), per_group("sn2_")]
+        logs = [per_group("log1_"), per_group("log2_")]
+        soft = [per_group("soft1_"), per_group("soft2_")]
+        sq = per_group("sq")
+        den = per_group("den")
+        log_den = per_group("log_den")
+        inv2 = per_group("inv2")
+        gate = per_group("gate")
+        num = per_group("num")
+        num2 = per_group("num2")
+        grad = per_group("grad")
+        res = per_group("res")
+        halves = [slice(h * HALF, (h + 1) * HALF) for h in range(2)]
+        last = G - 1
 
-        banks = [[ps.tile([P, N], F32, name="bank%d_%d" % (h, g)) for g in range(G)] for h in range(2)]
-        wide = [P, 2, 2, HALF]
-        flat = [P, 2, HALF]
-        sn = per_group("sn", wide)
-        logs = per_group("logs", wide)
-        soft = per_group("soft", wide)
-        sq = per_group("sq", flat)
-        den = per_group("den", flat)
-        log_den = per_group("log_den", flat)
-        inv2 = per_group("inv2", flat)
-        gate = per_group("gate", flat)
-        num = per_group("num", flat)
-        num2 = per_group("num2", flat)
-        grad = per_group("grad", flat)
-        res = per_group("res", flat)
-
-        def row(t):
-            return t.rearrange("p k c -> p (k c)")
-
-        parts = [slice(i * NT, (i + 1) * NT) for i in range(HALF // NT)]
-
-        def prepare_x(h):
-            x_bf, x_codes, x_scales = x_ops[h]
-            for cols in parts:
-                interleave(x_bf[:, cols, :], x_raw[h][:, :, cols])
-            for cols in parts:
-                quantize(x_codes[:, cols], x_scales[:, cols], x_bf[:, cols, :])
-
-        def forward(h, g, k):
-            for cols in parts:
-                dst = banks[h][g][:, k * HALF + cols.start : k * HALF + cols.stop]
-                product(dst, g, w_ops[k][1], w_ops[k][2], slice(0, M), x_ops[h][1], x_ops[h][2], cols)
-
-        def backward(g):
-            for i in range(N // NT):
-                cols = slice(i * NT, (i + 1) * NT)
-                product(banks[0][g][:, cols], g, wo_codes, wo_scales, slice(0, M), dy_codes, dy_scales, cols)
-
-        interleave(w_ops[0][0][:], w_raw[0][:])
-        quantize(w_ops[0][1][:], w_ops[0][2][:], w_ops[0][0][:])
-        prepare_x(0)
-        interleave(w_ops[1][0][:], w_raw[1][:])
-        quantize(w_ops[1][1][:], w_ops[1][2][:], w_ops[1][0][:])
-        for k in range(2):
+        for cols in halves:
+            interleave(nc.vector.tensor_copy, x_op, cols)
+        interleave(nc.scalar.copy, w1_op, w1_op["all"])
+        quantize(w1_op, w1_op["all"])
+        quantize(x_op, x_op["all"])
+        interleave(nc.vector.tensor_copy, w2_op, w2_op["all"])
+        interleave(nc.vector.tensor_copy, wo_op, wo_op["all"])
+        quantize(w2_op, w2_op["all"])
+        quantize(wo_op, wo_op["all"])
+        for k, weights in enumerate((w1_op, w2_op)):
             for g in range(G):
-                forward(0, g, k)
-                nc.scalar.activation(
-                    out=sn[g][:, 0, k, :], in_=banks[0][g][:, halves[k]], func=ACT.Sigmoid, scale=-1.0
-                )
-        prepare_x(1)
-        for g in range(G):
-            for k in range(2):
-                forward(1, g, k)
-            nc.scalar.activation(out=row(sn[g][:, 1]), in_=banks[1][g][:], func=ACT.Sigmoid, scale=-1.0)
-        interleave(wo_bf[:], wo_raw[:])
-        quantize(wo_codes[:], wo_scales[:], wo_bf[:])
+                product(banks[k][g], g, weights, x_op)
+                nc.scalar.activation(out=sn[k][g][:], in_=banks[k][g][:], func=ACT.Sigmoid, scale=-1.0)
         for cols in halves:
-            interleave(dy_bf[:, cols, :], dy_raw[:, :, cols])
+            interleave(nc.vector.tensor_copy, dy_op, cols)
         for cols in halves:
-            quantize(dy_codes[:, cols], dy_scales[:, cols], dy_bf[:, cols, :])
+            quantize(dy_op, cols)
         for g in range(G):
-            backward(g)
-
-        def take_log(g, h):
-            nc.scalar.activation(out=row(logs[g][:, h]), in_=row(sn[g][:, h]), func=ACT.Ln, bias=TINY)
-
-        def softplus(g, h):
-            z = banks[h][g][:]
+            product(banks[0][g], g, wo_op, dy_op)
+        for g in range(G):
             nc.vector.scalar_tensor_tensor(
-                out=row(soft[g][:, h]), in0=row(logs[g][:, h]), scalar=-1.0, in1=z, op0=ALU.mult, op1=ALU.max
+                out=gate[g][:], in0=sn[0][g][:], scalar=1.0, in1=banks[0][g][:], op0=ALU.subtract, op1=ALU.mult
             )
+            product(banks[0][g], g, w1_op, x_op)
 
-        def make_gate(g):
+        def softplus(g, k):
+            nc.scalar.activation(out=logs[k][g][:], in_=sn[k][g][:], func=ACT.Ln, bias=TINY)
             nc.vector.scalar_tensor_tensor(
-                out=gate[g][:], in0=sn[g][:, :, 0, :], scalar=1.0,
-                in1=banks[0][g][:].rearrange("p (h c) -> p h c", h=2), op0=ALU.subtract, op1=ALU.mult,
+                out=soft[k][g][:], in0=logs[k][g][:], scalar=-1.0, in1=banks[k][g][:], op0=ALU.mult, op1=ALU.max
             )
 
         def square(g):
-            nc.scalar.activation(out=sq[g][:], in_=soft[g][:, :, 0, :], func=ACT.Square)
+            nc.scalar.activation(out=sq[g][:], in_=soft[0][g][:], func=ACT.Square)
 
         def make_den(g):
             nc.vector.scalar_tensor_tensor(
-                out=den[g][:], in0=soft[g][:, :, 1, :], scalar=hp[:, g : g + 1], in1=sq[g][:],
-                op0=ALU.add, op1=ALU.add,
+                out=den[g][:], in0=soft[1][g][:], scalar=hp[:, g : g + 1], in1=sq[g][:], op0=ALU.add, op1=ALU.add
             )
 
         def take_log_den(g):
-            nc.scalar.activation(out=row(log_den[g][:]), in_=row(den[g][:]), func=ACT.Ln)
+            nc.scalar.activation(out=log_den[g][:], in_=den[g][:], func=ACT.Ln)
 
         def make_num(g, engine):
-            engine.tensor_tensor(out=num[g][:], in0=soft[g][:, :, 0, :], in1=gate[g][:], op=ALU.mult)
+            engine.tensor_tensor(out=num[g][:], in0=soft[0][g][:], in1=gate[g][:], op=ALU.mult)
 
         def make_num2(g):
             nc.vector.scalar_tensor_tensor(
-                out=num2[g][:], in0=soft[g][:, :, 1, :], scalar=hp[:, g : g + 1], in1=num[g][:],
-                op0=ALU.add, op1=ALU.mult,
+                out=num2[g][:], in0=soft[1][g][:], scalar=hp[:, g : g + 1], in1=num[g][:], op0=ALU.add, op1=ALU.mult
             )
 
         def inverse_square(g):
-            nc.scalar.activation(
-                out=row(inv2[g][:]), in_=row(log_den[g][:]), func=ACT.Exp, scale=-2.0, bias=math.log(4.0)
-            )
+            nc.scalar.activation(out=inv2[g][:], in_=log_den[g][:], func=ACT.Exp, scale=-2.0, bias=math.log(4.0))
 
         def make_grad(g):
-            nc.vector.tensor_tensor(out=row(grad[g][:]), in0=row(num2[g][:]), in1=row(inv2[g][:]), op=ALU.mult)
+            nc.vector.tensor_tensor(out=grad[g][:], in0=num2[g][:], in1=inv2[g][:], op=ALU.mult)
 
         def finish(g, cols):
-            nc.vector.tensor_tensor(
-                out=row(res[g][:])[:, cols], in0=old_sb[:, g, cols], in1=row(grad[g][:])[:, cols], op=ALU.subtract
-            )
-            nc.sync.dma_start(out=out[g, :, cols], in_=row(res[g][:])[:, cols])
+            nc.vector.tensor_tensor(out=res[g][:, cols], in0=old_sb[:, g, cols], in1=grad[g][:, cols], op=ALU.subtract)
+            nc.sync.dma_start(out=out[g, :, cols], in_=res[g][:, cols])
 
         for g in range(G):
-            make_gate(g)
-            for k in range(2):
-                forward(0, g, k)
-        last = G - 1
-        for g in range(G):
-            for h in (1, 0):
-                take_log(g, h)
-                softplus(g, h)
+            for k in (1, 0):
+                softplus(g, k)
             if g < last:
                 make_num(g, nc.gpsimd)
         for g in range(last):
             square(g)
-        nc.vector.tensor_tensor(
-            out=sq[last][:], in0=soft[last][:, :, 0, :], in1=soft[last][:, :, 0, :], op=ALU.mult
-        )
+        nc.vector.tensor_tensor(out=sq[last][:], in0=soft[0][last][:], in1=soft[0][last][:], op=ALU.mult)
         for g in range(G):
             make_den(g)
             take_log_den(g)
@@ -225,8 +170,8 @@ def tile_rows_bhill_kernel(tc, x, w1, w2, hp1, wo, dy, old, out):
             make_num2(g)
             inverse_square(g)
         make_grad(0)
-        for g in range(G - 1):
+        for g in range(last):
             make_grad(g + 1)
             finish(g, slice(0, N))
         for cols in halves:
-            finish(G - 1, cols)
+            finish(last, cols)

@@ -18,6 +18,7 @@ P = 128
 PACK = 4
 ROWS = D // PACK
 HALF = N // 2
+NT = 128
 RUN = 4
 TINY = 2.0 ** -44
 
@@ -37,29 +38,29 @@ def tile_rows_bhill_kernel(tc, x, w1, w2, hp1, wo, dy, old, out):
             packed = sb.tile([P, width, PACK], BF16, name=name + "_bf", align_bytes=64)
             codes = sb.tile([P, width], U32, name=name + "_codes", align_bytes=64)
             scales = sb.tile([P, width], U8, name=name + "_scales", align_bytes=64)
-            return {"raw": raw, "packed": packed, "codes": codes, "scales": scales, "all": slice(0, width)}
+            return {"raw": raw, "packed": packed, "codes": codes, "scales": scales}
 
-        def interleave(copy, op, cols):
-            copy(
-                out=op["packed"][:, cols, :].rearrange("p (c i) j -> p c j i", i=RUN),
-                in_=op["raw"][:, :, cols].rearrange("p j (c i) -> p c j i", i=RUN),
+        def interleave(operand, cols):
+            nc.vector.tensor_copy(
+                out=operand["packed"][:, cols, :].rearrange("p (c i) j -> p c j i", i=RUN),
+                in_=operand["raw"][:, :, cols].rearrange("p j (c i) -> p c j i", i=RUN),
             )
 
-        def quantize(op, cols):
+        def quantize(operand, cols):
             nc.vector.quantize_mx(
-                out=op["codes"][:, cols].bitcast(FP8X4),
-                scales=op["scales"][:, cols],
-                in_=op["packed"][:, cols, :].rearrange("p c j -> p (c j)"),
+                out=operand["codes"][:, cols].bitcast(FP8X4),
+                scales=operand["scales"][:, cols],
+                in_=operand["packed"][:, cols, :].rearrange("p c j -> p (c j)"),
             )
 
-        def product(bank, g, weights, moving):
+        def product(dst, g, weights, moving, cols):
             rows = slice(ROWS * g, ROWS * (g + 1))
             nc.tensor.matmul_mx(
-                out=bank[:],
+                out=dst,
                 lhsT=weights["codes"][rows, :].bitcast(FP8X4),
                 lhsT_scale=weights["scales"][rows, :],
-                rhs=moving["codes"][rows, :].bitcast(FP8X4),
-                rhs_scale=moving["scales"][rows, :],
+                rhs=moving["codes"][rows, cols].bitcast(FP8X4),
+                rhs_scale=moving["scales"][rows, cols],
                 start=True,
                 stop=True,
             )
@@ -67,111 +68,122 @@ def tile_rows_bhill_kernel(tc, x, w1, w2, hp1, wo, dy, old, out):
         def per_group(name):
             return [sb.tile([P, N], F32, name="%s%d" % (name, g)) for g in range(G)]
 
-        x_op = load("x", x)
-        w1_op = load("w1", w1)
-        w2_op = load("w2", w2)
-        wo_op = load("wo", wo)
-        dy_op = load("dy", dy)
+        features = slice(0, M)
+        whole = slice(0, N)
+        halves = [slice(h * HALF, (h + 1) * HALF) for h in range(2)]
+        calls = [slice(i * NT, (i + 1) * NT) for i in range(N // NT)]
+        calls_of_a_half = calls[: HALF // NT]
+        last = G - 1
+
+        w_mx, x_mx = [], []
+        for h, w in enumerate((w1, w2)):
+            w_mx.append(load("w%d" % (h + 1), w))
+            x_mx.append(load("x%d" % h, x[:, :, halves[h]]))
+        dy_mx = load("dy", dy)
+        wo_mx = load("wo", wo)
         hp = sb.tile([P, G], F32, name="hp")
         with nc.allow_non_contiguous_dma(reason="one half point to a partition"):
             nc.sync.dma_start(out=hp[:], in_=hp1.rearrange("g m one -> m (g one)"))
         old_sb = sb.tile([P, G, N], F32, name="old_sb")
         nc.sync.dma_start(out=old_sb[:], in_=old.rearrange("g m n -> m g n"))
 
-        banks = [[ps.tile([P, N], F32, name="bank%d_%d" % (k, g)) for g in range(G)] for k in range(2)]
-        sn = [per_group("sn1_"), per_group("sn2_")]
-        logs = [per_group("log1_"), per_group("log2_")]
+        banks = [[ps.tile([P, N], F32, name="bank%d_%d" % (r, g)) for g in range(G)] for r in range(2)]
+        sig_neg = [per_group("sig_neg1_"), per_group("sig_neg2_")]
+        log_sig = [per_group("log_sig1_"), per_group("log_sig2_")]
         soft = [per_group("soft1_"), per_group("soft2_")]
-        sq = per_group("sq")
+        gate = per_group("gate")
+        square = per_group("square")
         den = per_group("den")
         log_den = per_group("log_den")
-        inv2 = per_group("inv2")
-        gate = per_group("gate")
-        num = per_group("num")
-        num2 = per_group("num2")
-        grad = per_group("grad")
-        res = per_group("res")
-        halves = [slice(h * HALF, (h + 1) * HALF) for h in range(2)]
-        last = G - 1
+        inv_sq = per_group("inv_sq")
+        gate_s = per_group("gate_s")
+        gate_sb = per_group("gate_sb")
+        neg_dz = per_group("neg_dz")
+        result = per_group("result")
 
-        for cols in halves:
-            interleave(nc.vector.tensor_copy, x_op, cols)
-        interleave(nc.scalar.copy, w1_op, w1_op["all"])
-        quantize(w1_op, w1_op["all"])
-        quantize(x_op, x_op["all"])
-        interleave(nc.vector.tensor_copy, w2_op, w2_op["all"])
-        interleave(nc.vector.tensor_copy, wo_op, wo_op["all"])
-        quantize(w2_op, w2_op["all"])
-        quantize(wo_op, wo_op["all"])
-        for k, weights in enumerate((w1_op, w2_op)):
+        def forward(g, r, h):
+            for cols in calls_of_a_half:
+                dst = banks[r][g][:, h * HALF + cols.start : h * HALF + cols.stop]
+                product(dst, g, w_mx[r], x_mx[h], cols)
+
+        def sigmoids(r, h):
             for g in range(G):
-                product(banks[k][g], g, weights, x_op)
-                nc.scalar.activation(out=sn[k][g][:], in_=banks[k][g][:], func=ACT.Sigmoid, scale=-1.0)
+                forward(g, r, h)
+                nc.scalar.activation(
+                    out=sig_neg[r][g][:, halves[h]], in_=banks[r][g][:, halves[h]], func=ACT.Sigmoid, scale=-1.0
+                )
+
+        for h in range(2):
+            interleave(w_mx[h], features)
+            quantize(w_mx[h], features)
+            if h == 1:
+                sigmoids(1, 0)
+            for cols in calls_of_a_half:
+                interleave(x_mx[h], cols)
+            for cols in calls_of_a_half:
+                quantize(x_mx[h], cols)
+            sigmoids(0, h)
+        sigmoids(1, 1)
+
         for cols in halves:
-            interleave(nc.vector.tensor_copy, dy_op, cols)
-        for cols in halves:
-            quantize(dy_op, cols)
+            interleave(dy_mx, cols)
+        interleave(wo_mx, features)
+        quantize(dy_mx, halves[0])
+        quantize(wo_mx, features)
+        quantize(dy_mx, halves[1])
         for g in range(G):
-            product(banks[0][g], g, wo_op, dy_op)
+            for cols in calls:
+                product(banks[0][g][:, cols], g, wo_mx, dy_mx, cols)
         for g in range(G):
             nc.vector.scalar_tensor_tensor(
-                out=gate[g][:], in0=sn[0][g][:], scalar=1.0, in1=banks[0][g][:], op0=ALU.subtract, op1=ALU.mult
+                out=gate[g][:], in0=sig_neg[0][g][:], scalar=1.0, in1=banks[0][g][:], op0=ALU.subtract, op1=ALU.mult
             )
-            product(banks[0][g], g, w1_op, x_op)
+            for h in range(2):
+                forward(g, 0, h)
 
-        def softplus(g, k):
-            nc.scalar.activation(out=logs[k][g][:], in_=sn[k][g][:], func=ACT.Ln, bias=TINY)
+        for g in range(G):
+            for r in (1, 0):
+                nc.scalar.activation(out=log_sig[r][g][:], in_=sig_neg[r][g][:], func=ACT.Ln, bias=TINY)
+                nc.vector.scalar_tensor_tensor(
+                    out=soft[r][g][:], in0=log_sig[r][g][:], scalar=-1.0, in1=banks[r][g][:], op0=ALU.mult, op1=ALU.max
+                )
+
+        def times_s1(g):
+            nc.vector.tensor_tensor(out=gate_s[g][:], in0=soft[0][g][:], in1=gate[g][:], op=ALU.mult)
+
+        for g in range(G):
+            nc.scalar.activation(out=square[g][:], in_=soft[0][g][:], func=ACT.Square)
+        times_s1(0)
+        for g in range(G):
             nc.vector.scalar_tensor_tensor(
-                out=soft[k][g][:], in0=logs[k][g][:], scalar=-1.0, in1=banks[k][g][:], op0=ALU.mult, op1=ALU.max
+                out=den[g][:], in0=soft[1][g][:], scalar=hp[:, g : g + 1], in1=square[g][:], op0=ALU.add, op1=ALU.add
             )
-
-        def square(g):
-            nc.scalar.activation(out=sq[g][:], in_=soft[0][g][:], func=ACT.Square)
-
-        def make_den(g):
-            nc.vector.scalar_tensor_tensor(
-                out=den[g][:], in0=soft[1][g][:], scalar=hp[:, g : g + 1], in1=sq[g][:], op0=ALU.add, op1=ALU.add
-            )
-
-        def take_log_den(g):
             nc.scalar.activation(out=log_den[g][:], in_=den[g][:], func=ACT.Ln)
 
-        def make_num(g, engine):
-            engine.tensor_tensor(out=num[g][:], in0=soft[0][g][:], in1=gate[g][:], op=ALU.mult)
-
-        def make_num2(g):
+        for g in range(1, G):
+            times_s1(g)
+        for g in range(G):
             nc.vector.scalar_tensor_tensor(
-                out=num2[g][:], in0=soft[1][g][:], scalar=hp[:, g : g + 1], in1=num[g][:], op0=ALU.add, op1=ALU.mult
+                out=gate_sb[g][:], in0=soft[1][g][:], scalar=hp[:, g : g + 1], in1=gate_s[g][:],
+                op0=ALU.add, op1=ALU.mult,
             )
+            nc.scalar.activation(out=inv_sq[g][:], in_=log_den[g][:], func=ACT.Exp, scale=-2.0, bias=math.log(4.0))
 
-        def inverse_square(g):
-            nc.scalar.activation(out=inv2[g][:], in_=log_den[g][:], func=ACT.Exp, scale=-2.0, bias=math.log(4.0))
-
-        def make_grad(g):
-            nc.vector.tensor_tensor(out=grad[g][:], in0=num2[g][:], in1=inv2[g][:], op=ALU.mult)
+        def gradient(g, cols):
+            nc.vector.tensor_tensor(out=neg_dz[g][:, cols], in0=gate_sb[g][:, cols], in1=inv_sq[g][:, cols], op=ALU.mult)
 
         def finish(g, cols):
-            nc.vector.tensor_tensor(out=res[g][:, cols], in0=old_sb[:, g, cols], in1=grad[g][:, cols], op=ALU.subtract)
-            nc.sync.dma_start(out=out[g, :, cols], in_=res[g][:, cols])
+            nc.vector.tensor_tensor(
+                out=result[g][:, cols], in0=old_sb[:, g, cols], in1=neg_dz[g][:, cols], op=ALU.subtract
+            )
+            nc.sync.dma_start(out=out[g, :, cols], in_=result[g][:, cols])
 
-        for g in range(G):
-            for k in (1, 0):
-                softplus(g, k)
-            if g < last:
-                make_num(g, nc.gpsimd)
+        gradient(0, whole)
         for g in range(last):
-            square(g)
-        nc.vector.tensor_tensor(out=sq[last][:], in0=soft[0][last][:], in1=soft[0][last][:], op=ALU.mult)
-        for g in range(G):
-            make_den(g)
-            take_log_den(g)
-        make_num(last, nc.vector)
-        for g in range(G):
-            make_num2(g)
-            inverse_square(g)
-        make_grad(0)
-        for g in range(last):
-            make_grad(g + 1)
-            finish(g, slice(0, N))
+            if g + 1 < last:
+                gradient(g + 1, whole)
+            finish(g, whole)
+        for cols in halves:
+            gradient(last, cols)
         for cols in halves:
             finish(last, cols)

@@ -20,6 +20,7 @@ ROWS = D // PACK
 HALF = N // 2
 NT = 128
 RUN = 4
+GPSIMD_GROUPS = 2
 TINY = 2.0 ** -44
 
 
@@ -142,26 +143,24 @@ def tile_rows_bhill_kernel(tc, x, w1, w2, hp1, wo, dy, old, out):
                 forward(g, 0, h)
 
         for g in range(G):
-            for r in (1, 0):
+            for r in range(2):
                 nc.scalar.activation(out=log_sig[r][g][:], in_=sig_neg[r][g][:], func=ACT.Ln, bias=TINY)
                 nc.vector.scalar_tensor_tensor(
                     out=soft[r][g][:], in0=log_sig[r][g][:], scalar=-1.0, in1=banks[r][g][:], op0=ALU.mult, op1=ALU.max
                 )
-
-        def times_s1(g):
-            nc.vector.tensor_tensor(out=gate_s[g][:], in0=soft[0][g][:], in1=gate[g][:], op=ALU.mult)
+                if r == 0 and g < GPSIMD_GROUPS:
+                    nc.gpsimd.tensor_tensor(out=gate_s[g][:], in0=soft[0][g][:], in1=gate[g][:], op=ALU.mult)
 
         for g in range(G):
             nc.scalar.activation(out=square[g][:], in_=soft[0][g][:], func=ACT.Square)
-        times_s1(0)
         for g in range(G):
             nc.vector.scalar_tensor_tensor(
                 out=den[g][:], in0=soft[1][g][:], scalar=hp[:, g : g + 1], in1=square[g][:], op0=ALU.add, op1=ALU.add
             )
             nc.scalar.activation(out=log_den[g][:], in_=den[g][:], func=ACT.Ln)
 
-        for g in range(1, G):
-            times_s1(g)
+        for g in range(GPSIMD_GROUPS, G):
+            nc.vector.tensor_tensor(out=gate_s[g][:], in0=soft[0][g][:], in1=gate[g][:], op=ALU.mult)
         for g in range(G):
             nc.vector.scalar_tensor_tensor(
                 out=gate_sb[g][:], in0=soft[1][g][:], scalar=hp[:, g : g + 1], in1=gate_s[g][:],

from contextlib import ExitStack
import math

import concourse.mybir as mybir

G, D, M, N = 4, 128, 128, 512
FLOPS = 3 * 2 * G * D * M * N

F32 = mybir.dt.float32
BF16 = mybir.dt.bfloat16
U32 = mybir.dt.uint32
U8 = mybir.dt.uint8
FP8X4 = mybir.dt.float8_e4m3fn_x4
ACT = mybir.ActivationFunctionType
ALU = mybir.AluOpType

P = 128
PACK = 4
ROWS = D // PACK
HALF = N // 2
NT = 128
RUN = 4
GPSIMD_GROUPS = 2
TINY = 2.0 ** -44


def tile_rows_bhill_kernel(tc, x, w1, w2, hp1, wo, dy, old, out):
    nc = tc.nc

    with ExitStack() as ctx:
        sb = ctx.enter_context(tc.tile_pool(name="sb", bufs=1))
        ps = ctx.enter_context(tc.psum_pool(name="ps", bufs=1))
        ctx.enter_context(tc.manual_schedule())

        def load(name, src):
            width = src.shape[2]
            raw = sb.tile([P, PACK, width], F32, name=name + "_raw")
            nc.sync.dma_start(out=raw[:], in_=src.rearrange("g (p j) c -> (g p) j c", j=PACK))
            packed = sb.tile([P, width, PACK], BF16, name=name + "_bf", align_bytes=64)
            codes = sb.tile([P, width], U32, name=name + "_codes", align_bytes=64)
            scales = sb.tile([P, width], U8, name=name + "_scales", align_bytes=64)
            return {"raw": raw, "packed": packed, "codes": codes, "scales": scales}

        def interleave(operand, cols):
            nc.vector.tensor_copy(
                out=operand["packed"][:, cols, :].rearrange("p (c i) j -> p c j i", i=RUN),
                in_=operand["raw"][:, :, cols].rearrange("p j (c i) -> p c j i", i=RUN),
            )

        def quantize(operand, cols):
            nc.vector.quantize_mx(
                out=operand["codes"][:, cols].bitcast(FP8X4),
                scales=operand["scales"][:, cols],
                in_=operand["packed"][:, cols, :].rearrange("p c j -> p (c j)"),
            )

        def product(dst, g, weights, moving, cols):
            rows = slice(ROWS * g, ROWS * (g + 1))
            nc.tensor.matmul_mx(
                out=dst,
                lhsT=weights["codes"][rows, :].bitcast(FP8X4),
                lhsT_scale=weights["scales"][rows, :],
                rhs=moving["codes"][rows, cols].bitcast(FP8X4),
                rhs_scale=moving["scales"][rows, cols],
                start=True,
                stop=True,
            )

        def per_group(name):
            return [sb.tile([P, N], F32, name="%s%d" % (name, g)) for g in range(G)]

        features = slice(0, M)
        whole = slice(0, N)
        halves = [slice(h * HALF, (h + 1) * HALF) for h in range(2)]
        calls = [slice(i * NT, (i + 1) * NT) for i in range(N // NT)]
        calls_of_a_half = calls[: HALF // NT]
        last = G - 1

        w_mx, x_mx = [], []
        for h, w in enumerate((w1, w2)):
            w_mx.append(load("w%d" % (h + 1), w))
            x_mx.append(load("x%d" % h, x[:, :, halves[h]]))
        dy_mx = load("dy", dy)
        wo_mx = load("wo", wo)
        hp = sb.tile([P, G], F32, name="hp")
        with nc.allow_non_contiguous_dma(reason="one half point to a partition"):
            nc.sync.dma_start(out=hp[:], in_=hp1.rearrange("g m one -> m (g one)"))
        old_sb = sb.tile([P, G, N], F32, name="old_sb")
        nc.sync.dma_start(out=old_sb[:], in_=old.rearrange("g m n -> m g n"))

        banks = [[ps.tile([P, N], F32, name="bank%d_%d" % (r, g)) for g in range(G)] for r in range(2)]
        sig_neg = [per_group("sig_neg1_"), per_group("sig_neg2_")]
        log_sig = [per_group("log_sig1_"), per_group("log_sig2_")]
        soft = [per_group("soft1_"), per_group("soft2_")]
        gate = per_group("gate")
        square = per_group("square")
        den = per_group("den")
        log_den = per_group("log_den")
        inv_sq = per_group("inv_sq")
        gate_s = per_group("gate_s")
        gate_sb = per_group("gate_sb")
        neg_dz = per_group("neg_dz")
        result = per_group("result")

        def forward(g, r, h):
            for cols in calls_of_a_half:
                dst = banks[r][g][:, h * HALF + cols.start : h * HALF + cols.stop]
                product(dst, g, w_mx[r], x_mx[h], cols)

        def sigmoids(r, h):
            for g in range(G):
                forward(g, r, h)
                nc.scalar.activation(
                    out=sig_neg[r][g][:, halves[h]], in_=banks[r][g][:, halves[h]], func=ACT.Sigmoid, scale=-1.0
                )

        for h in range(2):
            interleave(w_mx[h], features)
            quantize(w_mx[h], features)
            if h == 1:
                sigmoids(1, 0)
            for cols in calls_of_a_half:
                interleave(x_mx[h], cols)
            for cols in calls_of_a_half:
                quantize(x_mx[h], cols)
            sigmoids(0, h)
        sigmoids(1, 1)

        for cols in halves:
            interleave(dy_mx, cols)
        interleave(wo_mx, features)
        quantize(dy_mx, halves[0])
        quantize(wo_mx, features)
        quantize(dy_mx, halves[1])
        for g in range(G):
            for cols in calls:
                product(banks[0][g][:, cols], g, wo_mx, dy_mx, cols)
        for g in range(G):
            nc.vector.scalar_tensor_tensor(
                out=gate[g][:], in0=sig_neg[0][g][:], scalar=1.0, in1=banks[0][g][:], op0=ALU.subtract, op1=ALU.mult
            )
            for h in range(2):
                forward(g, 0, h)

        for g in range(G):
            for r in range(2):
                nc.scalar.activation(out=log_sig[r][g][:], in_=sig_neg[r][g][:], func=ACT.Ln, bias=TINY)
                nc.vector.scalar_tensor_tensor(
                    out=soft[r][g][:], in0=log_sig[r][g][:], scalar=-1.0, in1=banks[r][g][:], op0=ALU.mult, op1=ALU.max
                )
                if r == 0 and g < GPSIMD_GROUPS:
                    nc.gpsimd.tensor_tensor(out=gate_s[g][:], in0=soft[0][g][:], in1=gate[g][:], op=ALU.mult)

        for g in range(G):
            nc.scalar.activation(out=square[g][:], in_=soft[0][g][:], func=ACT.Square)
        for g in range(G):
            nc.vector.scalar_tensor_tensor(
                out=den[g][:], in0=soft[1][g][:], scalar=hp[:, g : g + 1], in1=square[g][:], op0=ALU.add, op1=ALU.add
            )
            nc.scalar.activation(out=log_den[g][:], in_=den[g][:], func=ACT.Ln)

        for g in range(GPSIMD_GROUPS, G):
            nc.vector.tensor_tensor(out=gate_s[g][:], in0=soft[0][g][:], in1=gate[g][:], op=ALU.mult)
        for g in range(G):
            nc.vector.scalar_tensor_tensor(
                out=gate_sb[g][:], in0=soft[1][g][:], scalar=hp[:, g : g + 1], in1=gate_s[g][:],
                op0=ALU.add, op1=ALU.mult,
            )
            nc.scalar.activation(out=inv_sq[g][:], in_=log_den[g][:], func=ACT.Exp, scale=-2.0, bias=math.log(4.0))

        def gradient(g, cols):
            nc.vector.tensor_tensor(out=neg_dz[g][:, cols], in0=gate_sb[g][:, cols], in1=inv_sq[g][:, cols], op=ALU.mult)

        def finish(g, cols):
            nc.vector.tensor_tensor(
                out=result[g][:, cols], in0=old_sb[:, g, cols], in1=neg_dz[g][:, cols], op=ALU.subtract
            )
            nc.sync.dma_start(out=out[g, :, cols], in_=result[g][:, cols])

        gradient(0, whole)
        for g in range(last):
            if g + 1 < last:
                gradient(g + 1, whole)
            finish(g, whole)
        for cols in halves:
            gradient(last, cols)
        for cols in halves:
            finish(last, cols)
